import numpy as np
import ml_dtypes


def mxq(x, axis, fmt="e4m3"):
    dtype, down = {"e4m3": (ml_dtypes.float8_e4m3fn, 7), "e5m2": (ml_dtypes.float8_e5m2, 14)}[fmt]
    v = np.moveaxis(np.asarray(x, np.float32).astype(ml_dtypes.bfloat16).astype(np.float64), axis, -1)
    blocks = v.reshape(v.shape[:-1] + (-1, 32))
    amax = np.abs(blocks).max(-1, keepdims=True)
    byte = np.maximum(np.where(amax > 0, np.frexp(amax)[1] - 1 + 127, 0) - down, 1)
    scale = np.exp2(byte - 127.0)
    codes = (blocks / scale).astype(np.float32).astype(dtype).astype(np.float64)
    return np.moveaxis((codes * scale).reshape(v.shape), -1, axis)


WIDE = False


def mx_kscale(k):
    if not WIDE:
        return np.ones(k)
    levels = np.array([30, -30])
    if k % 512:
        return np.exp2(np.random.permutation(np.resize(levels, k // 32))).repeat(32)
    a = np.empty((k // 512, 16))
    for p in range(k // 512):
        a[p, :8] = np.random.permutation(np.resize(levels, 8))
        for g in range(8):
            far = levels[np.abs(levels - a[p, g]) >= 10]
            a[p, g + 8] = far[np.random.randint(len(far))]
    return np.exp2(a.ravel()).repeat(32)


def f64(x):
    return np.asarray(x).astype(np.float64)


def striped(idx):
    return np.tile(np.asarray(idx).reshape(-1, 16).T, (8, 1)).astype(np.uint16)


def unstriped(offs):
    return offs[:16].T.reshape(-1).astype(np.int64)


E2M1 = np.array([0.0, 0.5, 1.0, 1.5, 2.0, 3.0, 4.0, 6.0, -0.0, -0.5, -1.0, -1.5, -2.0, -3.0, -4.0, -6.0])


def pack_weight(w, fmt):
    k, n = w.shape
    w = f64(np.asarray(w, np.float32).astype(ml_dtypes.bfloat16)).reshape(k // 32, 32, n)
    amax = np.abs(w).max(1)
    if fmt in ("e4m3", "e5m2"):
        byte = np.frexp(amax)[1] - 1 + 127 - (7 if fmt == "e4m3" else 14)
    else:
        mant, ex = np.frexp(amax / 6.0)
        byte = np.where(mant > 0.5, ex, ex - 1) + 127
    byte = np.clip(np.where(amax > 0, byte, 1), 1, 254)
    scaled = (w * np.exp2(127.0 - byte)[:, None, :]).reshape(k, n).astype(np.float32)
    by_word = np.ascontiguousarray(scaled.reshape(k // 512, 128, 4, n).transpose(0, 1, 3, 2))
    if fmt in ("e4m3", "e5m2"):
        words = by_word.astype(ml_dtypes.float8_e4m3fn if fmt == "e4m3" else ml_dtypes.float8_e5m2).view(np.uint8)
    else:
        c = by_word.astype(ml_dtypes.float4_e2m1fn).view(np.uint8) & 0xF
        words = (c[..., 0::2] | (c[..., 1::2] << 4)).reshape(k // 512, 128, 2 * n)
    return np.ascontiguousarray(words), np.ascontiguousarray(byte.astype(np.uint8).reshape(k // 512, 16, n))


def unpack_weight(words, scales, fmt):
    g, _, n = scales.shape
    words = np.ascontiguousarray(words).reshape(g, 128, n, -1)
    if fmt in ("e4m3", "e5m2"):
        vals = words.view(ml_dtypes.float8_e4m3fn if fmt == "e4m3" else ml_dtypes.float8_e5m2).astype(np.float64)
    else:
        nib = np.empty((g, 128, n, 4), np.uint8)
        nib[..., 0::2] = words & 0xF
        nib[..., 1::2] = words >> 4
        vals = E2M1[nib]
    vals = vals * np.repeat(np.exp2(scales.astype(np.float64) - 127.0), 8, axis=1)[..., None]
    return vals.transpose(0, 1, 3, 2).reshape(g * 512, n)


def sigmoid(v):
    return 1.0 / (1.0 + np.exp(-v))


K, F, T, Z, J, R, C, O, N, E = 512, 512, 1024, 1024, 256, 512, 512, 256, 256, 1024


def setup_inputs():
    n = np.random.standard_normal
    idx = np.random.permutation(T)[:J]
    idx2 = np.random.permutation(Z)[:J]
    idx3 = np.random.permutation(C)[:J]
    idx4 = np.random.permutation(C)[:J]
    idx5 = np.random.permutation(C)[:O]
    idx6 = np.random.permutation(C)[:O]
    idx7 = np.random.permutation(E)[:O]
    fk = mx_kscale(K)
    fr = mx_kscale(R)
    ff = mx_kscale(F)
    xtp = pack_weight(n((K, T)) / fk[:, None], "e2m1")
    wp = pack_weight(n((K, R)) * 1 / np.sqrt(K) * fk[:, None] * fr, "e5m2")
    xop = pack_weight(n((F, Z)) / ff[:, None], "e5m2")
    w2p = pack_weight(n((F, R)) * 1 / np.sqrt(F) * ff[:, None] * fr, "e4m3")
    wbp = pack_weight(n((R, N)) * 1 / np.sqrt(R) / fr[:, None], "e4m3")
    return {
        "xt_words": xtp[0],
        "xt_scales": xtp[1],
        "w_words": wp[0],
        "w_scales": wp[1],
        "xo_words": xop[0],
        "xo_scales": xop[1],
        "w2_words": w2p[0],
        "w2_scales": w2p[1],
        "wb_words": wbp[0],
        "wb_scales": wbp[1],
        "tz": (n((N, E))).astype(np.float32),
        "so": (np.random.uniform(0.6, 1.6, (N, 1))).astype(np.float32),
        "bo": (np.random.uniform(-1.0, 1.0, (N, 1))).astype(np.float32),
        "offs": striped(idx),
        "offs2": striped(idx2),
        "offs3": striped(idx3),
        "offs4": striped(idx4),
        "offs5": striped(idx5),
        "offs6": striped(idx6),
        "offs7": striped(idx7),
    }


def reference(xt_words, xt_scales, w_words, w_scales, xo_words, xo_scales, w2_words, w2_scales, wb_words, wb_scales, tz, so, bo, offs, offs2, offs3, offs4, offs5, offs6, offs7):
    idx = unstriped(offs)
    idx2 = unstriped(offs2)
    idx3 = unstriped(offs3)
    idx4 = unstriped(offs4)
    idx5 = unstriped(offs5)
    idx6 = unstriped(offs6)
    idx7 = unstriped(offs7)
    xtu = unpack_weight(xt_words, xt_scales, "e2m1")
    wu = unpack_weight(w_words, w_scales, "e5m2")
    xou = unpack_weight(xo_words, xo_scales, "e5m2")
    w2u = unpack_weight(w2_words, w2_scales, "e4m3")
    wbu = unpack_weight(wb_words, wb_scales, "e4m3")
    xtidxg = xtu[:, idx]
    a = wu.T @ xtidxg
    xoidx2g = xou[:, idx2]
    b = w2u.T @ xoidx2g
    pw = np.zeros((R, C))
    pw[:, idx3] = a
    pv = np.zeros((R, C))
    pv[:, idx4] = b
    hid = np.maximum(pw[:, idx5], pv[:, idx6])
    hidq = mxq(hid, 0, "e5m2")
    p = wbu.T @ hidq
    y = p * sigmoid(f64(tz)[:, idx7] * f64(so) + f64(bo))
    return y

from contextlib import ExitStack

import concourse.mybir as mybir

K, F, T, Z, J, R, C, O, N, E = 512, 512, 1024, 1024, 256, 512, 512, 256, 256, 1024
FLOPS = 2 * (K * R * J + F * R * J + R * N * O)

F32 = mybir.dt.float32
BF16 = mybir.dt.bfloat16
I32 = mybir.dt.int32
U32 = mybir.dt.uint32
U16 = mybir.dt.uint16
U8 = mybir.dt.uint8
E2M1 = mybir.dt.float4_e2m1fn_x4
E4M3 = mybir.dt.float8_e4m3fn_x4
E5M2 = mybir.dt.float8_e5m2_x4
ACT = mybir.ActivationFunctionType
ALU = mybir.AluOpType

P = 128
PACK = 4
QUAD = 32
HALVES = N // P


def tile_list_twotab_twoboards_one_finalgate_kernel(
    tc, xt_words, xt_scales, w_words, w_scales, xo_words, xo_scales, w2_words, w2_scales,
    wb_words, wb_scales, tz, so, bo, offs, offs2, offs3, offs4, offs5, offs6, offs7, out,
):
    nc = tc.nc
    with ExitStack() as ctx:
        lists = ctx.enter_context(tc.tile_pool(name="lists", bufs=1))
        sb = ctx.enter_context(tc.tile_pool(name="sb", bufs=1))
        ps1 = ctx.enter_context(tc.psum_pool(name="ps1", bufs=6))
        ps2 = ctx.enter_context(tc.psum_pool(name="ps2", bufs=2))

        def new(name, shape, dtype):
            return sb.tile(shape, dtype, name=name, align_bytes=64)

        def load_list(name, src):
            tile = lists.tile([P, J // 16], U16, name=name)
            nc.sync.dma_start(tile[:], src)
            return tile

        def load_words(queue, name, src, columns, dtype):
            tile = new(name, [P, columns], dtype)
            queue.dma_start(tile[:].bitcast(I32), src.bitcast(I32))
            return tile

        def load_scales(queue, tile, src, quadrants):
            for q in quadrants:
                rows = src[0, PACK * q : PACK * (q + 1), :].bitcast(I32)
                queue.dma_start(tile[QUAD * q : QUAD * (q + 1), :].bitcast(I32), rows.partition_broadcast(QUAD // PACK))

        def flat(words):
            return words[0].rearrange("p n t -> p (n t)")

        xt_s, w_s, xo_s, w2_s, wb_s = (
            new(name, [P, columns], U8)
            for name, columns in (("xt_s", T), ("w_s", R), ("xo_s", Z), ("w2_s", R), ("wb_s", N))
        )
        l1 = load_list("l1", offs)
        load_scales(nc.scalar, xt_s, xt_scales, range(4))
        load_scales(nc.sync, w_s, w_scales, range(1))
        xt_w = load_words(nc.sync, "xt_w", xt_words[0], T, U16)
        w_w = load_words(nc.sync, "w_w", flat(w_words), R, U32)
        load_scales(nc.sync, w_s, w_scales, range(1, 4))
        l3 = load_list("l3", offs3)
        l2 = load_list("l2", offs2)
        xo_w = load_words(nc.sync, "xo_w", flat(xo_words), Z, U32)
        w2_w = load_words(nc.sync, "w2_w", flat(w2_words), R, U32)
        load_scales(nc.sync, xo_s, xo_scales, range(4))
        load_scales(nc.sync, w2_s, w2_scales, range(4))
        l4 = load_list("l4", offs4)
        l5 = load_list("l5", offs5)
        l6 = load_list("l6", offs6)
        tz_t = []
        for h in range(HALVES):
            tile = new("tz%d" % h, [P, E], F32)
            nc.sync.dma_start(tile[:], tz[P * h : P * (h + 1), :])
            tz_t.append(tile)
        l7 = load_list("l7", offs7)
        so_t = new("so_t", [P, HALVES], F32)
        bo_t = new("bo_t", [P, HALVES], F32)
        with nc.allow_non_contiguous_dma(reason="one value a partition"):
            nc.sync.dma_start(so_t[:], so.rearrange("(h p) o -> p (h o)", p=P))
            nc.sync.dma_start(bo_t[:], bo.rearrange("(h p) o -> p (h o)", p=P))
        wb_w = load_words(nc.sync, "wb_w", flat(wb_words), N, U32)
        load_scales(nc.sync, wb_s, wb_scales, range(4))

        boards = {}
        for s, engine in (("a", nc.vector), ("b", nc.gpsimd)):
            for t in range(PACK):
                boards[s, t] = new("board_%s%d" % (s, t), [P, C], F32)
                engine.memset(boards[s, t][:], 0.0)

        def pick(name, table, offsets, dtype):
            picked = new(name, [P, J], dtype)
            nc.vector.tensor_copy(picked[:], table[:].indirect(offsets[:]))
            return picked

        def deal(dst, src, slots):
            nc.vector.tensor_copy(
                dst[:].rearrange("p (t m) -> p t m", t=PACK)[:, slots, :],
                src[:].rearrange("p (m t) -> p t m", t=PACK)[:, slots, :],
            )

        def product(s, t, on_scalar, dw, ds, wfmt, gw, gs, xfmt, offsets):
            acc = ps1.tile([P, J], F32, name="acc1")
            cols = slice(P * t, P * (t + 1))
            nc.tensor.matmul_mx(acc[:], lhsT=dw[:, cols].bitcast(wfmt), lhsT_scale=ds[:, cols],
                                rhs=gw[:].bitcast(xfmt), rhs_scale=gs[:], start=True, stop=True)
            vals = new("vals_%s%d" % (s, t), [P, J], F32)
            place = boards[s, t][:].indirect(offsets[:])
            if on_scalar:
                nc.scalar.copy(vals[:], acc[:])
                nc.scalar.activation(place, vals[:], ACT.Copy)
            else:
                nc.vector.tensor_copy(vals[:], acc[:])
                nc.vector.tensor_copy(place, vals[:])

        read = {s: new("read_" + s, [P, PACK, O], F32) for s in "ab"}

        def fetch(s, t, on_scalar, offsets):
            window = boards[s, t][:].indirect(offsets[:])
            if on_scalar:
                nc.scalar.activation(read[s][:, t, :], window, ACT.Copy)
            else:
                nc.vector.tensor_copy(read[s][:, t, :], window)

        wd_w, vd_w = new("wd_w", [P, R], U32), new("vd_w", [P, R], U32)
        wd_s, vd_s = new("wd_s", [P, R], U8), new("vd_s", [P, R], U8)
        xg_w = pick("xg_w", xt_w, l1, U16)
        xg_s = pick("xg_s", xt_s, l1, U8)
        for slots in (slice(0, 1), slice(1, PACK)):
            deal(wd_w, w_w, slots)
            deal(wd_s, w_s, slots)

        def prod_a(t, on_scalar):
            product("a", t, on_scalar, wd_w, wd_s, E5M2, xg_w, xg_s, E2M1, l3)

        def prod_b(t, on_scalar):
            product("b", t, on_scalar, vd_w, vd_s, E4M3, og_w, og_s, E5M2, l4)

        prod_a(0, True)
        og_w = pick("og_w", xo_w, l2, U32)
        deal(vd_w, w2_w, slice(0, PACK))
        prod_a(1, False)
        prod_a(2, True)
        og_s = pick("og_s", xo_s, l2, U8)
        deal(vd_s, w2_s, slice(0, PACK))
        prod_a(3, True)
        prod_b(0, False)
        prod_b(1, True)
        prod_b(2, False)
        prod_b(3, False)
        for t in range(PACK):
            fetch("a", t, True, l5)
        for t in range(PACK):
            fetch("b", t, t < 2, l6)

        gate = []
        for h in range(HALVES):
            tile = new("gate%d" % h, [P, O], F32)
            nc.scalar.activation(tile[:], tz_t[h][:].indirect(l7[:]), ACT.Sigmoid,
                                 bias=bo_t[:, h : h + 1], scale=so_t[:, h : h + 1])
            gate.append(tile)

        hid = new("hid", [P, O, PACK], BF16)
        hq_w = new("hq_w", [P, O], U32)
        hq_s = new("hq_s", [P, O], U8)
        half = O // 2
        for u in range(2):
            cols = slice(half * u, half * (u + 1))
            nc.vector.tensor_tensor(
                hid[:, cols, :].rearrange("p (c i) t -> p c t i", i=4),
                read["a"][:, :, cols].rearrange("p t (c i) -> p c t i", i=4),
                read["b"][:, :, cols].rearrange("p t (c i) -> p c t i", i=4),
                ALU.max,
            )
        for u in range(2):
            cols = slice(half * u, half * (u + 1))
            nc.vector.quantize_mx(hq_w[:, cols].bitcast(E5M2), hq_s[:, cols],
                                  hid[:, cols, :].rearrange("p o t -> p (o t)"))
        for h in range(HALVES):
            acc = ps2.tile([P, O], F32, name="acc2")
            cols = slice(P * h, P * (h + 1))
            nc.tensor.matmul_mx(acc[:], lhsT=wb_w[:, cols].bitcast(E4M3), lhsT_scale=wb_s[:, cols],
                                rhs=hq_w[:].bitcast(E5M2), rhs_scale=hq_s[:], start=True, stop=True)
            res = new("res%d" % h, [P, O], F32)
            nc.vector.tensor_tensor(res[:], acc[:], gate[h][:], ALU.mult)
            (nc.sync, nc.scalar)[h].dma_start(out[cols, :], res[:])
